import numpy as np
import ml_dtypes


def mxq(x, axis, fmt="e4m3"):
    dtype, down = {"e4m3": (ml_dtypes.float8_e4m3fn, 7), "e5m2": (ml_dtypes.float8_e5m2, 14)}[fmt]
    v = np.moveaxis(np.asarray(x, np.float32).astype(ml_dtypes.bfloat16).astype(np.float64), axis, -1)
    blocks = v.reshape(v.shape[:-1] + (-1, 32))
    amax = np.abs(blocks).max(-1, keepdims=True)
    byte = np.maximum(np.where(amax > 0, np.frexp(amax)[1] - 1 + 127, 0) - down, 1)
    scale = np.exp2(byte - 127.0)
    codes = (blocks / scale).astype(np.float32).astype(dtype).astype(np.float64)
    return np.moveaxis((codes * scale).reshape(v.shape), -1, axis)


WIDE = False


def mx_kscale(k):
    if not WIDE:
        return np.ones(k)
    levels = np.array([10, -10, 5, -5, 0])
    if k % 512:
        return np.exp2(np.random.permutation(np.resize(levels, k // 32))).repeat(32)
    a = np.empty((k // 512, 16))
    for p in range(k // 512):
        a[p, :8] = np.random.permutation(np.resize(levels, 8))
        for g in range(8):
            far = levels[np.abs(levels - a[p, g]) >= 10]
            a[p, g + 8] = far[np.random.randint(len(far))]
    return np.exp2(a.ravel()).repeat(32)


BF16 = ml_dtypes.bfloat16


def bf(x):
    return np.asarray(x, np.float32).astype(BF16)


def f64(x):
    return np.asarray(x).astype(np.float64)


P, Q, S, R, D = 1024, 1024, 512, 512, 1024

X_MAX = 0.5
C_LOCAL = 3.0


def contrast(u):
    x = X_MAX * np.tanh(u)
    return C_LOCAL * x / (1.0 - x)


def draw0():
    s, r, t = mx_kscale(Q), mx_kscale(R), mx_kscale(P)
    return {"g_re": bf(0.5 * np.random.standard_normal((P, Q)) / np.sqrt(Q) * s * t[:, None]),
            "g_im": bf(0.5 * np.random.standard_normal((P, Q)) / np.sqrt(Q) * s * t[:, None]),
            "j": bf(np.random.standard_normal((Q, S)) / s[:, None]),
            "e0_re": bf(0.5 * np.random.standard_normal((P, S)) * t[:, None]),
            "e0_im": bf(0.5 * np.random.standard_normal((P, S)) * t[:, None]),
            "phi": bf(np.random.uniform(-1.5, 1.5, (P,))),
            "a": bf(np.random.standard_normal((D, R)) * r),
            "b": bf(np.random.standard_normal((R, P)) / np.sqrt(R) / r[:, None]),
            "host": bf(0.3 * np.random.standard_normal((P,))),
            "vol": bf((1.0 + 0.1 * np.random.standard_normal((P,))) / np.sqrt(np.sqrt(P)) / t)}


def core(g_re, g_im, j, e0_re, e0_im, phi, a, b, host, vol):
    jq = mxq(f64(j), 0, "e4m3")
    t_re = f64(e0_re) + (mxq(f64(g_re), 1, "e4m3") @ jq)
    t_im = f64(e0_im) + (mxq(f64(g_im), 1, "e4m3") @ jq)
    c = np.cos(f64(phi))[:, None]
    d = np.sin(f64(phi))[:, None]
    f_re = c * t_re - d * t_im
    f_im = d * t_re + c * t_im
    u = (mxq(f64(a), 1, "e4m3") @ mxq(f64(b), 0, "e4m3")) + f64(host)
    chi = contrast(u) * f64(vol)
    chiq = mxq(chi, 1, "e4m3")
    m_re = chiq @ mxq(f_re, 0, "e4m3")
    m_im = chiq @ mxq(f_im, 0, "e4m3")
    return m_re, m_im


def e4m3fn_bytes(y):
    return np.clip(np.asarray(y, np.float64), -448.0, 448.0).astype(np.float32).astype(ml_dtypes.float8_e4m3fn).view(np.uint8)


def e4m3fn_values(b):
    return np.asarray(b, np.uint8).view(ml_dtypes.float8_e4m3fn).astype(np.float64)


def setup_inputs():
    d = draw0()
    x0 = np.asarray(d['j']).astype(np.float64)
    s = (np.max(np.abs(x0), axis=(1,), keepdims=True) / 448.0).astype(np.float32)
    out = {}
    for k, v in d.items():
        if k == 'j':
            out['j_bytes'] = e4m3fn_bytes(x0 / s.astype(np.float64))
            out['j_scale'] = s
        else:
            out[k] = v
    return out


def reference(g_re, g_im, j_bytes, j_scale, e0_re, e0_im, phi, a, b, host, vol):
    return core(g_re, g_im, e4m3fn_values(j_bytes) * j_scale.astype(np.float64), e0_re, e0_im, phi, a, b, host, vol)

@@ -1,0 +1,448 @@
+import math
+from contextlib import ExitStack
+
+import concourse.mybir as mybir
+from concourse.masks import make_identity
+
+P, Q, S, R, D = 1024, 1024, 512, 512, 1024
+FLOPS = 2 * (2 * P * Q * S + D * R * P + 2 * D * P * S)
+
+F32 = mybir.dt.float32
+BF16 = mybir.dt.bfloat16
+U32 = mybir.dt.uint32
+U8 = mybir.dt.uint8
+FP8 = mybir.dt.float8_e4m3fn
+FP8X4 = mybir.dt.float8_e4m3fn_x4
+ALU = mybir.AluOpType
+ACT = mybir.ActivationFunctionType
+
+N = 128
+RE, IM = 0, 1
+
+
+def tile_green_material_moments_f5_kernel(
+    tc, g_re, g_im, j_bytes, j_scale, e0_re, e0_im, phi, a, b, host, vol, out_0, out_1
+):
+    nc = tc.nc
+    with ExitStack() as ctx:
+        keep = ctx.enter_context(tc.tile_pool(name="keep", bufs=1))
+        work = ctx.enter_context(tc.tile_pool(name="work", bufs=2))
+        psum = ctx.enter_context(tc.psum_pool(name="psum", bufs=4))
+        ctx.enter_context(tc.manual_schedule())
+
+        js = keep.tile([N, 2, 4], F32, name="js")
+        nc.scalar.dma_start(out=js[:], in_=j_scale.rearrange("(g p t) o -> p g (t o)", g=2, p=N))
+        phi_sb = keep.tile([N, 2, 4], BF16, name="phi_sb")
+        nc.scalar.dma_start(out=phi_sb[:], in_=phi.rearrange("(g p t) -> p g t", g=2, p=N))
+        host_sb = keep.tile([N, 2, 4], BF16, name="host_sb")
+        nc.scalar.dma_start(out=host_sb[:], in_=host.rearrange("(g p t) -> p g t", g=2, p=N))
+        vol_sb = keep.tile([N, 2, 4], BF16, name="vol_sb")
+        nc.scalar.dma_start(out=vol_sb[:], in_=vol.rearrange("(g p t) -> p g t", g=2, p=N))
+
+        jb_view = j_bytes.rearrange("(g p t) n -> g p t n", p=N, t=4)
+        jb = []
+        for g in range(2):
+            tile = keep.tile([N, 4, S], U8, name=f"jb{g}", align_bytes=64)
+            jb.append(tile)
+            nc.sync.dma_start(out=tile[:], in_=jb_view[g])
+
+        g_view = [x.rearrange("(g p t) q -> g p t q", p=N, t=4) for x in (g_re, g_im)]
+        e_view = [x.rearrange("(g p t) s -> g p t s", p=N, t=4) for x in (e0_re, e0_im)]
+        g_sb = [[keep.tile([N, 4, Q], BF16, name=f"g{g}{c}", align_bytes=64) for c in range(2)] for g in range(2)]
+        e_sb = [[keep.tile([N, 4, S], BF16, name=f"e{g}{c}", align_bytes=64) for c in range(2)] for g in range(2)]
+        a_sb = keep.tile([N, 4, 2, R], BF16, name="a_sb", align_bytes=64)
+        b_sb = keep.tile([N, 4, P], BF16, name="b_sb", align_bytes=64)
+
+        def load_g(g, t0, t1):
+            for c in range(2):
+                nc.sync.dma_start(out=g_sb[g][c][:, t0:t1, :], in_=g_view[c][g][:, t0:t1, :])
+
+        def load_e(g):
+            for c in range(2):
+                nc.sync.dma_start(out=e_sb[g][c][:], in_=e_view[c][g])
+
+        load_g(0, 0, 1)
+        load_g(0, 1, 2)
+        load_e(0)
+        load_g(0, 2, 4)
+        nc.sync.dma_start(out=b_sb[:], in_=b.rearrange("(p j) w -> p j w", j=4))
+        load_g(1, 0, 2)
+        load_e(1)
+        load_g(1, 2, 4)
+        nc.sync.dma_start(out=a_sb[:], in_=a.rearrange("(c p e) r -> p c e r", c=4, p=N))
+
+        ident = keep.tile([N, N], F32, name="ident")
+        make_identity(nc, ident[:])
+        zero = keep.tile([N, 1], F32, name="zero")
+        nc.vector.memset(zero[:], 0.0)
+        dummy = keep.tile([N, 2], F32, name="dummy")
+        nc.scalar.activation(out=dummy[:, 0:1], in_=zero[:], func=ACT.Sin)
+
+        angle = keep.tile([N, 3, 8], F32, name="angle")
+        trig = keep.tile([N, 3, 8], F32, name="trig")
+        mag = keep.tile([N, 8], F32, name="mag")
+        bias_u = keep.tile([N, 8], F32, name="bias_u")
+        vol1 = keep.tile([N, 8], F32, name="vol1")
+        vol2 = keep.tile([N, 8], F32, name="vol2")
+        phi_flat = phi_sb[:].rearrange("p g t -> p (g t)")
+        host_flat = host_sb[:].rearrange("p g t -> p (g t)")
+        vol_flat = vol_sb[:].rearrange("p g t -> p (g t)")
+        nc.vector.tensor_copy(out=angle[:, 0, :], in_=phi_flat)
+        nc.vector.tensor_scalar(out=angle[:, 2, :], in0=phi_flat, scalar1=-1.0, scalar2=None, op0=ALU.mult)
+        nc.vector.tensor_tensor(out=mag[:], in0=angle[:, 0, :], in1=angle[:, 2, :], op=ALU.max)
+        nc.vector.tensor_scalar(
+            out=angle[:, 1, :], in0=mag[:], scalar1=-1.0, scalar2=math.pi / 2, op0=ALU.mult, op1=ALU.add
+        )
+        nc.scalar.activation(
+            out=trig[:].rearrange("p k c -> p (k c)"), in_=angle[:].rearrange("p k c -> p (k c)"), func=ACT.Sin
+        )
+        nc.scalar.activation(out=dummy[:, 1:2], in_=zero[:], func=ACT.Tanh)
+
+        def sin_col(i):
+            return trig[:, 0, i : i + 1]
+
+        def cos_col(i):
+            return trig[:, 1, i : i + 1]
+
+        def neg_sin_col(i):
+            return trig[:, 2, i : i + 1]
+
+        def planes_tile(name):
+            return work.tile([N, 4, S], BF16, name=name, tag="planes", bufs=4, align_bytes=64)
+
+        def woven_tile(name):
+            return work.tile([N, S, 4], BF16, name=name, tag="woven", bufs=4, align_bytes=64)
+
+        jw = [planes_tile(f"jw{g}") for g in range(2)]
+        j_codes = keep.tile([N, 2 * S], U32, name="j_codes", align_bytes=64)
+        j_planes = keep.tile([N, 2 * S], U8, name="j_planes", align_bytes=64)
+        jg = [woven_tile(f"jg{g}") for g in range(2)]
+
+        def widen_v(g, t):
+            nc.vector.tensor_scalar(
+                out=jw[g][:, t, :], in0=jb[g][:, t, :].bitcast(FP8), scalar1=js[:, g, t : t + 1],
+                scalar2=None, op0=ALU.mult,
+            )
+
+        def widen_s(g, t):
+            nc.scalar.activation(
+                out=jw[g][:, t, :], in_=jb[g][:, t, :].bitcast(FP8), func=ACT.Copy, scale=js[:, g, t : t + 1]
+            )
+
+        def weave(copy, dst, src, c0, c1):
+            copy(
+                out=dst[:, c0:c1, :].rearrange("p (c i) t -> p c t i", i=4),
+                in_=src[:, :, c0:c1].rearrange("p t (c i) -> p c t i", i=4),
+            )
+
+        def quantize(codes, planes, grouped):
+            nc.vector.quantize_mx(out=codes.bitcast(FP8X4), scales=planes, in_=grouped)
+
+        def matmul(out, lhs, rhs, first, last):
+            nc.tensor.matmul_mx(
+                out=out, lhsT=lhs[0].bitcast(FP8X4), lhsT_scale=lhs[1], rhs=rhs[0].bitcast(FP8X4), rhs_scale=rhs[1],
+                start=first, stop=last,
+            )
+
+        banks_t = {}
+        grouped_g = {}
+        codes_g = {}
+        banks_f = {}
+        tot = {}
+        prod = {}
+        fw = {}
+        fg = {}
+        f_codes = [[keep.tile([N, S], U32, name=f"fc{g}{c}", align_bytes=64) for c in range(2)] for g in range(2)]
+        f_planes = [[keep.tile([N, S], U8, name=f"fp{g}{c}", align_bytes=64) for c in range(2)] for g in range(2)]
+
+        def turn(i):
+            g, t = divmod(i, 4)
+            for c in range(2):
+                bank = psum.tile([N, 4, N], F32, name=f"turn{i}{c}", tag="turn", bufs=4)
+                banks_t[i, c] = bank
+                words = g_sb[g][c][:, t, :].bitcast(F32)
+                for k in range(2):
+                    for u in range(2):
+                        nc.tensor.transpose(bank[:, 2 * k + u, :], words[:, 256 * k + u : 256 * (k + 1) : 2], ident[:])
+
+        def regroup(i, c, copy):
+            if c == 0:
+                grouped_g[i] = work.tile([N, 2, 2 * N * 4], BF16, name=f"gg{i}", tag="gg", bufs=3, align_bytes=64)
+            copy(
+                out=grouped_g[i][:, c, :].bitcast(F32).rearrange("p (k r u) -> p k r u", k=2, u=2),
+                in_=banks_t[i, c][:].rearrange("p (k u) r -> p k r u", k=2),
+            )
+
+        def quantize_g(i):
+            codes = work.tile([N, 4 * N], U32, name=f"gc{i}", tag="gc", bufs=3, align_bytes=64)
+            planes = work.tile([N, 4 * N], U8, name=f"gp{i}", tag="gp", bufs=3, align_bytes=64)
+            codes_g[i] = (codes, planes)
+            quantize(codes[:], planes[:], grouped_g[i][:].rearrange("p c w -> p (c w)"))
+
+        def field(i):
+            codes, planes = codes_g[i]
+            for c in range(2):
+                bank = psum.tile([N, S], F32, name=f"field{i}{c}", tag="acc", bufs=4)
+                banks_f[i, c] = bank
+                for k in range(2):
+                    w = slice((2 * c + k) * N, (2 * c + k + 1) * N)
+                    m = slice(k * S, (k + 1) * S)
+                    matmul(bank[:], (codes[:, w], planes[:, w]), (j_codes[:, m], j_planes[:, m]), k == 0, k == 1)
+
+        def add_e(i, c):
+            g, t = divmod(i, 4)
+            tile = work.tile([N, S], F32, name=f"t{i}{c}", tag=f"t{c}", bufs=3)
+            tot[i, c] = tile
+            nc.vector.tensor_tensor(out=tile[:], in0=banks_f[i, c][:], in1=e_sb[g][c][:, t, :], op=ALU.add)
+
+        def scale_re(i):
+            for c, col in ((RE, cos_col(i)), (IM, sin_col(i))):
+                tile = work.tile([N, S], F32, name=f"q{i}{c}", tag=f"q{c}", bufs=3)
+                prod[i, c] = tile
+                nc.scalar.activation(out=tile[:], in_=tot[i, RE][:], func=ACT.Copy, scale=col)
+
+        def rotate(i):
+            g, t = divmod(i, 4)
+            for c, col in ((RE, neg_sin_col(i)), (IM, cos_col(i))):
+                if t == 0:
+                    fw[g, c] = planes_tile(f"fw{g}{c}")
+                nc.vector.scalar_tensor_tensor(
+                    out=fw[g, c][:, t, :], in0=tot[i, IM][:], scalar=col, in1=prod[i, c][:], op0=ALU.mult, op1=ALU.add
+                )
+
+        def weave_f(g, c, copy, c0, c1):
+            if c0 == 0:
+                fg[g, c] = woven_tile(f"fg{g}{c}")
+            weave(copy, fg[g, c], fw[g, c], c0, c1)
+
+        def quantize_f(g, c):
+            quantize(f_codes[g][c][:], f_planes[g][c][:], fg[g, c][:].rearrange("p s t -> p (s t)"))
+
+        bg = [keep.tile([N, 4, N, 4], BF16, name=f"bg{g}", align_bytes=64) for g in range(2)]
+        b_codes = [keep.tile([N, 4 * N], U32, name=f"bc{g}", align_bytes=64) for g in range(2)]
+        b_planes = [keep.tile([N, 4 * N], U8, name=f"bp{g}", align_bytes=64) for g in range(2)]
+
+        def weave_b(g, copy, t0, t1):
+            copy(
+                out=bg[g][:, t0:t1],
+                in_=b_sb[:, :, 512 * g : 512 * (g + 1)].rearrange("p j (m t) -> p t m j", t=4)[:, t0:t1],
+            )
+
+        def quantize_b(g):
+            quantize(b_codes[g][:], b_planes[g][:], bg[g][:].rearrange("p t m j -> p (t m j)"))
+
+        banks_a = {}
+        grouped_a = {}
+        codes_a = {}
+
+        def turn_a(c):
+            bank = psum.tile([N, 4, N], F32, name=f"turna{c}", tag="turn", bufs=4)
+            banks_a[c] = bank
+            for e in range(2):
+                words = a_sb[:, c, e, :].bitcast(F32)
+                for u in range(2):
+                    nc.tensor.transpose(bank[:, 2 * e + u, :], words[:, u:256:2], ident[:])
+
+        def regroup_a(c, copy):
+            tile = work.tile([N, 2 * N * 4], BF16, name=f"ag{c}", tag="ag", bufs=2, align_bytes=64)
+            grouped_a[c] = tile
+            copy(
+                out=tile[:].bitcast(F32).rearrange("p (e r u) -> p e r u", e=2, u=2),
+                in_=banks_a[c][:].rearrange("p (e u) r -> p e r u", e=2),
+            )
+
+        def quantize_a(c):
+            codes = keep.tile([N, 2 * N], U32, name=f"ac{c}", align_bytes=64)
+            planes = keep.tile([N, 2 * N], U8, name=f"ap{c}", align_bytes=64)
+            codes_a[c] = (codes, planes)
+            quantize(codes[:], planes[:], grouped_a[c][:])
+
+        banks_u = {}
+        th = {}
+        cw = {}
+        cg = {}
+        codes_c = {}
+
+        def material(c, g):
+            codes, planes = codes_a[c]
+            for h in range(2):
+                bank = psum.tile([N, 2, 2 * N], F32, name=f"u{c}{g}{h}", tag="turn", bufs=4)
+                banks_u[c, g, h] = bank
+                for e in range(2):
+                    w = slice((2 * h + e) * N, (2 * h + e + 1) * N)
+                    matmul(bank[:, e, :], (b_codes[g][:, w], b_planes[g][:, w]), (codes[:], planes[:]), True, True)
+
+        def tanh_u(c, g):
+            tile = work.tile([N, 4, 2 * N], F32, name=f"th{c}{g}", tag="th", bufs=3)
+            th[c, g] = tile
+            for t in range(4):
+                nc.scalar.activation(
+                    out=tile[:, t, :], in_=banks_u[c, g, t // 2][:, t % 2, :], func=ACT.Tanh,
+                    bias=bias_u[:, 4 * g + t : 4 * g + t + 1],
+                )
+
+        def affine(c, g):
+            tile = work.tile([N, 4, 2 * N], BF16, name=f"cw{c}{g}", tag="cw", bufs=3, align_bytes=64)
+            cw[c, g] = tile
+            for t in range(4):
+                i = 4 * g + t
+                nc.vector.tensor_scalar(
+                    out=tile[:, t, :], in0=th[c, g][:, t, :], scalar1=vol2[:, i : i + 1], scalar2=vol1[:, i : i + 1],
+                    op0=ALU.mult, op1=ALU.add,
+                )
+
+        def weave_c(c, g, copy):
+            tile = work.tile([N, 2 * N, 4], BF16, name=f"cg{c}{g}", tag="cg", bufs=3, align_bytes=64)
+            cg[c, g] = tile
+            weave(copy, tile, cw[c, g], 0, 2 * N)
+
+        def quantize_c(c, g):
+            codes = keep.tile([N, 2 * N], U32, name=f"cc{c}{g}", align_bytes=64)
+            planes = keep.tile([N, 2 * N], U8, name=f"cp{c}{g}", align_bytes=64)
+            codes_c[c, g] = (codes, planes)
+            quantize(codes[:], planes[:], cg[c, g][:].rearrange("p s t -> p (s t)"))
+
+        banks_m = {}
+        res = {}
+        out_view = [x.rearrange("(c p e) s -> c p e s", p=N, e=2) for x in (out_0, out_1)]
+
+        def moment(c, e, k):
+            bank = psum.tile([N, S], F32, name=f"m{c}{e}{k}", tag="acc", bufs=4)
+            banks_m[c, e, k] = bank
+            w = slice(e * N, (e + 1) * N)
+            for g in range(2):
+                codes, planes = codes_c[c, g]
+                matmul(bank[:], (codes[:, w], planes[:, w]), (f_codes[g][k][:], f_planes[g][k][:]), g == 0, g == 1)
+
+        def empty(c, e, k, copy):
+            if e == 0:
+                res[c, k] = work.tile([N, 2, S], F32, name=f"res{c}{k}", tag=f"res{k}", bufs=2)
+            copy(out=res[c, k][:, e, :], in_=banks_m[c, e, k][:])
+
+        def store(c, k):
+            nc.sync.dma_start(out=out_view[k][c], in_=res[c, k][:])
+
+        V, A = nc.vector.tensor_copy, nc.scalar.copy
+
+        for t in range(4):
+            widen_v(0, t)
+        turn(0)
+        turn(1)
+        regroup(0, RE, A)
+        regroup(0, IM, A)
+        weave(V, jg[0], jw[0], 0, S)
+        widen_v(1, 0)
+        widen_v(1, 1)
+        widen_s(1, 2)
+        widen_s(1, 3)
+        regroup(1, RE, A)
+        regroup(1, IM, A)
+        quantize(j_codes[:, :S], j_planes[:, :S], jg[0][:].rearrange("p s t -> p (s t)"))
+        weave(V, jg[1], jw[1], 0, S)
+        quantize_g(0)
+        quantize(j_codes[:, S:], j_planes[:, S:], jg[1][:].rearrange("p s t -> p (s t)"))
+        nc.vector.tensor_scalar(
+            out=bias_u[:], in0=host_flat, scalar1=-0.5 * math.log(3.0), scalar2=None, op0=ALU.add
+        )
+        nc.vector.tensor_scalar(out=vol2[:], in0=vol_flat, scalar1=2.0, scalar2=None, op0=ALU.mult)
+        nc.vector.tensor_copy(out=vol1[:], in_=vol_flat)
+        field(0)
+        turn(2)
+
+        def step(i):
+            if i < 7:
+                quantize_g(i + 1)
+                field(i + 1)
+            if i + 3 < 8:
+                turn(i + 3)
+            if i < 8:
+                add_e(i, RE)
+                add_e(i, IM)
+            if i >= 1:
+                scale_re(i - 1)
+            if i + 2 < 8:
+                regroup(i + 2, RE, A)
+                regroup(i + 2, IM, A)
+            if i >= 1:
+                rotate(i - 1)
+
+        step(0)
+        step(1)
+        weave_b(0, A, 0, 2)
+        step(2)
+        weave_b(0, A, 2, 4)
+        step(3)
+        weave_b(1, A, 0, 2)
+        quantize_b(0)
+        step(4)
+        weave_b(1, A, 2, 4)
+        weave_f(0, RE, V, 0, S // 2)
+        turn_a(0)
+        turn_a(1)
+        step(5)
+        quantize_b(1)
+        weave_f(0, RE, A, S // 2, S)
+        regroup_a(0, A)
+        regroup_a(1, A)
+        quantize_a(0)
+        material(0, 0)
+        step(6)
+        quantize_a(1)
+        quantize_f(0, RE)
+        weave_f(0, IM, V, 0, S // 2)
+        tanh_u(0, 0)
+        material(0, 1)
+        weave_f(0, IM, A, S // 2, S)
+        step(7)
+        affine(0, 0)
+        tanh_u(0, 1)
+        quantize_f(0, IM)
+        weave_c(0, 0, V)
+        step(8)
+        affine(0, 1)
+        quantize_c(0, 0)
+        weave_f(1, RE, V, 0, S)
+        turn_a(2)
+        turn_a(3)
+        regroup_a(2, A)
+        regroup_a(3, A)
+        weave_f(1, IM, V, 0, S)
+        quantize_f(1, RE)
+        material(1, 0)
+        tanh_u(1, 0)
+        weave_c(0, 1, V)
+        quantize_f(1, IM)
+        quantize_a(2)
+        material(1, 1)
+        tanh_u(1, 1)
+        quantize_c(0, 1)
+        quantize_a(3)
+
+        for c in range(4):
+            last = c == 3
+            moment(c, 0, RE)
+            moment(c, 0, IM)
+            moment(c, 1, RE)
+            moment(c, 1, IM)
+            if not last:
+                affine(c + 1, 0)
+                affine(c + 1, 1)
+                weave_c(c + 1, 0, V)
+            if c + 2 < 4:
+                material(c + 2, 0)
+            empty(c, 0, RE, A)
+            empty(c, 0, IM, V if last else A)
+            if not last:
+                weave_c(c + 1, 1, V)
+                quantize_c(c + 1, 0)
+            if c + 2 < 4:
+                tanh_u(c + 2, 0)
+                material(c + 2, 1)
+            empty(c, 1, RE, A)
+            store(c, RE)
+            empty(c, 1, IM, V if last else A)
+            store(c, IM)
+            if not last:
+                quantize_c(c + 1, 1)
+            if c + 2 < 4:
+                tanh_u(c + 2, 1)

@@ -16,8 +16,14 @@ FP8X4 = mybir.dt.float8_e4m3fn_x4
 ALU = mybir.AluOpType
 ACT = mybir.ActivationFunctionType
 
-N = 128
+LANES = 128
+PACK = 4
+PASS = LANES * PACK
+HALVES = P // PASS
+TILES = P // LANES
 RE, IM = 0, 1
+
+CHUNKS = ((0, 1, 2, 3), (4, 5), (6, 7))
 
 
 def tile_green_material_moments_f5_kernel(
@@ -30,113 +36,145 @@ def tile_green_material_moments_f5_kernel(
         psum = ctx.enter_context(tc.psum_pool(name="psum", bufs=4))
         ctx.enter_context(tc.manual_schedule())
 
-        js = keep.tile([N, 2, 4], F32, name="js")
-        nc.scalar.dma_start(out=js[:], in_=j_scale.rearrange("(g p t) o -> p g (t o)", g=2, p=N))
-        phi_sb = keep.tile([N, 2, 4], BF16, name="phi_sb")
-        nc.scalar.dma_start(out=phi_sb[:], in_=phi.rearrange("(g p t) -> p g t", g=2, p=N))
-        host_sb = keep.tile([N, 2, 4], BF16, name="host_sb")
-        nc.scalar.dma_start(out=host_sb[:], in_=host.rearrange("(g p t) -> p g t", g=2, p=N))
-        vol_sb = keep.tile([N, 2, 4], BF16, name="vol_sb")
-        nc.scalar.dma_start(out=vol_sb[:], in_=vol.rearrange("(g p t) -> p g t", g=2, p=N))
+        def load_cells(source, dtype, name):
+            tile = keep.tile([LANES, TILES], dtype, name=name)
+            nc.scalar.dma_start(
+                out=tile[:].rearrange("p (g t) -> p g t", t=PACK),
+                in_=source.rearrange("(g p t) -> p g t", p=LANES, t=PACK),
+            )
+            return tile
 
-        jb_view = j_bytes.rearrange("(g p t) n -> g p t n", p=N, t=4)
-        jb = []
-        for g in range(2):
-            tile = keep.tile([N, 4, S], U8, name=f"jb{g}", align_bytes=64)
-            jb.append(tile)
-            nc.sync.dma_start(out=tile[:], in_=jb_view[g])
+        scale_j = load_cells(j_scale.rearrange("k o -> (k o)"), F32, "scale_j")
+        phi_sb = load_cells(phi, BF16, "phi_sb")
+        host_sb = load_cells(host, BF16, "host_sb")
+        vol_sb = load_cells(vol, BF16, "vol_sb")
 
-        g_view = [x.rearrange("(g p t) q -> g p t q", p=N, t=4) for x in (g_re, g_im)]
-        e_view = [x.rearrange("(g p t) s -> g p t s", p=N, t=4) for x in (e0_re, e0_im)]
-        g_sb = [[keep.tile([N, 4, Q], BF16, name=f"g{g}{c}", align_bytes=64) for c in range(2)] for g in range(2)]
-        e_sb = [[keep.tile([N, 4, S], BF16, name=f"e{g}{c}", align_bytes=64) for c in range(2)] for g in range(2)]
-        a_sb = keep.tile([N, 4, 2, R], BF16, name="a_sb", align_bytes=64)
-        b_sb = keep.tile([N, 4, P], BF16, name="b_sb", align_bytes=64)
+        def four_rows(source):
+            return source.rearrange("(g p t) n -> g p t n", p=LANES, t=PACK)
+
+        j_raw = [keep.tile([LANES, PACK, S], U8, name=f"j_raw{g}", align_bytes=64) for g in range(HALVES)]
+        g_sb = [
+            [keep.tile([LANES, PACK, Q], BF16, name=f"g_sb{g}{c}", align_bytes=64) for c in (RE, IM)]
+            for g in range(HALVES)
+        ]
+        e_sb = [
+            [keep.tile([LANES, PACK, S], BF16, name=f"e_sb{g}{c}", align_bytes=64) for c in (RE, IM)]
+            for g in range(HALVES)
+        ]
+        a_sb = keep.tile([LANES, D // LANES, R], BF16, name="a_sb", align_bytes=64)
+        b_sb = keep.tile([LANES, PACK, P], BF16, name="b_sb", align_bytes=64)
+
+        def load_rows(tiles, sources, g, t0, t1):
+            for c in (RE, IM):
+                nc.sync.dma_start(out=tiles[g][c][:, t0:t1, :], in_=four_rows(sources[c])[g][:, t0:t1, :])
 
         def load_g(g, t0, t1):
-            for c in range(2):
-                nc.sync.dma_start(out=g_sb[g][c][:, t0:t1, :], in_=g_view[c][g][:, t0:t1, :])
+            load_rows(g_sb, (g_re, g_im), g, t0, t1)
 
-        def load_e(g):
-            for c in range(2):
-                nc.sync.dma_start(out=e_sb[g][c][:], in_=e_view[c][g])
+        def load_e(g, t0, t1):
+            load_rows(e_sb, (e0_re, e0_im), g, t0, t1)
 
+        def load_b(g):
+            w = slice(g * PASS, (g + 1) * PASS)
+            nc.sync.dma_start(out=b_sb[:, :, w], in_=four_rows(b)[0][:, :, w])
+
+        def load_a(n0, n1):
+            nc.sync.dma_start(out=a_sb[:, n0:n1, :], in_=a.rearrange("(n p) r -> p n r", p=LANES)[:, n0:n1, :])
+
+        for g in range(HALVES):
+            nc.sync.dma_start(out=j_raw[g][:], in_=four_rows(j_bytes)[g])
         load_g(0, 0, 1)
         load_g(0, 1, 2)
-        load_e(0)
-        load_g(0, 2, 4)
-        nc.sync.dma_start(out=b_sb[:], in_=b.rearrange("(p j) w -> p j w", j=4))
-        load_g(1, 0, 2)
-        load_e(1)
+        load_e(0, 0, 2)
+        load_g(0, 2, 3)
+        load_b(0)
+        load_b(1)
+        load_g(0, 3, 4)
+        load_a(0, 4)
+        load_e(0, 2, 4)
+        load_g(1, 0, 1)
+        load_g(1, 1, 2)
+        load_e(1, 0, 2)
         load_g(1, 2, 4)
-        nc.sync.dma_start(out=a_sb[:], in_=a.rearrange("(c p e) r -> p c e r", c=4, p=N))
+        load_e(1, 2, 4)
+        load_a(4, 8)
 
-        ident = keep.tile([N, N], F32, name="ident")
+        ident = keep.tile([LANES, LANES], F32, name="ident")
         make_identity(nc, ident[:])
-        zero = keep.tile([N, 1], F32, name="zero")
-        nc.vector.memset(zero[:], 0.0)
-        dummy = keep.tile([N, 2], F32, name="dummy")
-        nc.scalar.activation(out=dummy[:, 0:1], in_=zero[:], func=ACT.Sin)
 
-        angle = keep.tile([N, 3, 8], F32, name="angle")
-        trig = keep.tile([N, 3, 8], F32, name="trig")
-        mag = keep.tile([N, 8], F32, name="mag")
-        bias_u = keep.tile([N, 8], F32, name="bias_u")
-        vol1 = keep.tile([N, 8], F32, name="vol1")
-        vol2 = keep.tile([N, 8], F32, name="vol2")
-        phi_flat = phi_sb[:].rearrange("p g t -> p (g t)")
-        host_flat = host_sb[:].rearrange("p g t -> p (g t)")
-        vol_flat = vol_sb[:].rearrange("p g t -> p (g t)")
-        nc.vector.tensor_copy(out=angle[:, 0, :], in_=phi_flat)
-        nc.vector.tensor_scalar(out=angle[:, 2, :], in0=phi_flat, scalar1=-1.0, scalar2=None, op0=ALU.mult)
-        nc.vector.tensor_tensor(out=mag[:], in0=angle[:, 0, :], in1=angle[:, 2, :], op=ALU.max)
+        zero = keep.tile([LANES, 1], F32, name="zero")
+        first_use = keep.tile([LANES, 2], F32, name="first_use")
+        nc.vector.memset(zero[:], 0.0)
+        nc.scalar.activation(out=first_use[:, 0:1], in_=zero[:], func=ACT.Sin)
+
+        angle = keep.tile([LANES, 3, TILES], F32, name="angle")
+        trig = keep.tile([LANES, 3, TILES], F32, name="trig")
+        magnitude = keep.tile([LANES, TILES], F32, name="magnitude")
+        nc.vector.tensor_copy(out=angle[:, 0, :], in_=phi_sb[:])
+        nc.vector.tensor_scalar(out=angle[:, 2, :], in0=phi_sb[:], scalar1=-1.0, scalar2=None, op0=ALU.mult)
+        nc.vector.tensor_tensor(out=magnitude[:], in0=angle[:, 0, :], in1=angle[:, 2, :], op=ALU.max)
         nc.vector.tensor_scalar(
-            out=angle[:, 1, :], in0=mag[:], scalar1=-1.0, scalar2=math.pi / 2, op0=ALU.mult, op1=ALU.add
+            out=angle[:, 1, :], in0=magnitude[:], scalar1=-1.0, scalar2=math.pi / 2, op0=ALU.mult, op1=ALU.add
         )
         nc.scalar.activation(
-            out=trig[:].rearrange("p k c -> p (k c)"), in_=angle[:].rearrange("p k c -> p (k c)"), func=ACT.Sin
+            out=trig[:].rearrange("p k i -> p (k i)"), in_=angle[:].rearrange("p k i -> p (k i)"), func=ACT.Sin
         )
-        nc.scalar.activation(out=dummy[:, 1:2], in_=zero[:], func=ACT.Tanh)
+        nc.scalar.activation(out=first_use[:, 1:2], in_=zero[:], func=ACT.Tanh)
 
-        def sin_col(i):
-            return trig[:, 0, i : i + 1]
+        def column(tile, i):
+            return tile[:, i : i + 1]
 
-        def cos_col(i):
-            return trig[:, 1, i : i + 1]
+        def sine(i):
+            return column(trig[:, 0, :], i)
 
-        def neg_sin_col(i):
-            return trig[:, 2, i : i + 1]
+        def cosine(i):
+            return column(trig[:, 1, :], i)
 
-        def planes_tile(name):
-            return work.tile([N, 4, S], BF16, name=name, tag="planes", bufs=4, align_bytes=64)
+        def minus_sine(i):
+            return column(trig[:, 2, :], i)
+
+        tanh_bias = keep.tile([LANES, TILES], F32, name="tanh_bias")
+        vol_1 = keep.tile([LANES, TILES], F32, name="vol_1")
+        vol_2 = keep.tile([LANES, TILES], F32, name="vol_2")
+
+        def material_constants():
+            nc.vector.tensor_scalar(
+                out=tanh_bias[:], in0=host_sb[:], scalar1=-0.5 * math.log(3.0), scalar2=None, op0=ALU.add
+            )
+            nc.vector.tensor_scalar(out=vol_2[:], in0=vol_sb[:], scalar1=2.0, scalar2=None, op0=ALU.mult)
+            nc.vector.tensor_copy(out=vol_1[:], in_=vol_sb[:])
+
+        VECTOR, SCALAR = nc.vector.tensor_copy, nc.scalar.copy
+
+        def rows_tile(name):
+            return work.tile([LANES, PACK, S], BF16, name=name, tag="rows", bufs=4, align_bytes=64)
 
         def woven_tile(name):
-            return work.tile([N, S, 4], BF16, name=name, tag="woven", bufs=4, align_bytes=64)
+            return work.tile([LANES, S, PACK], BF16, name=name, tag="woven", bufs=4, align_bytes=64)
 
-        jw = [planes_tile(f"jw{g}") for g in range(2)]
-        j_codes = keep.tile([N, 2 * S], U32, name="j_codes", align_bytes=64)
-        j_planes = keep.tile([N, 2 * S], U8, name="j_planes", align_bytes=64)
-        jg = [woven_tile(f"jg{g}") for g in range(2)]
-
-        def widen_v(g, t):
-            nc.vector.tensor_scalar(
-                out=jw[g][:, t, :], in0=jb[g][:, t, :].bitcast(FP8), scalar1=js[:, g, t : t + 1],
-                scalar2=None, op0=ALU.mult,
-            )
-
-        def widen_s(g, t):
-            nc.scalar.activation(
-                out=jw[g][:, t, :], in_=jb[g][:, t, :].bitcast(FP8), func=ACT.Copy, scale=js[:, g, t : t + 1]
-            )
-
-        def weave(copy, dst, src, c0, c1):
+        def weave(copy, woven, rows, n0, n1):
             copy(
-                out=dst[:, c0:c1, :].rearrange("p (c i) t -> p c t i", i=4),
-                in_=src[:, :, c0:c1].rearrange("p t (c i) -> p c t i", i=4),
+                out=woven[:, n0:n1, :].rearrange("p (n i) t -> p n t i", i=4),
+                in_=rows[:, :, n0:n1].rearrange("p t (n i) -> p n t i", i=4),
             )
 
-        def quantize(codes, planes, grouped):
-            nc.vector.quantize_mx(out=codes.bitcast(FP8X4), scales=planes, in_=grouped)
+        def half_row(h):
+            return h * S // 2, (h + 1) * S // 2
+
+        def quantized_pair(columns, name):
+            return (
+                keep.tile([LANES, columns], U32, name=f"{name}_codes", align_bytes=64),
+                keep.tile([LANES, columns], U8, name=f"{name}_scales", align_bytes=64),
+            )
+
+        def cut(pair, w):
+            return pair[0][:, w], pair[1][:, w]
+
+        def everything(pair):
+            return pair[0][:], pair[1][:]
+
+        def quantize(pair, woven):
+            nc.vector.quantize_mx(out=pair[0].bitcast(FP8X4), scales=pair[1], in_=woven)
 
         def matmul(out, lhs, rhs, first, last):
             nc.tensor.matmul_mx(
@@ -144,305 +182,324 @@ def tile_green_material_moments_f5_kernel(
                 start=first, stop=last,
             )
 
-        banks_t = {}
-        grouped_g = {}
-        codes_g = {}
-        banks_f = {}
-        tot = {}
-        prod = {}
-        fw = {}
-        fg = {}
-        f_codes = [[keep.tile([N, S], U32, name=f"fc{g}{c}", align_bytes=64) for c in range(2)] for g in range(2)]
-        f_planes = [[keep.tile([N, S], U8, name=f"fp{g}{c}", align_bytes=64) for c in range(2)] for g in range(2)]
+        j_rows = [rows_tile(f"j_rows{g}") for g in range(HALVES)]
+        j_woven = [woven_tile(f"j_woven{g}") for g in range(HALVES)]
+        j_mx = quantized_pair(HALVES * S, "j")
 
-        def turn(i):
-            g, t = divmod(i, 4)
-            for c in range(2):
-                bank = psum.tile([N, 4, N], F32, name=f"turn{i}{c}", tag="turn", bufs=4)
-                banks_t[i, c] = bank
-                words = g_sb[g][c][:, t, :].bitcast(F32)
-                for k in range(2):
-                    for u in range(2):
-                        nc.tensor.transpose(bank[:, 2 * k + u, :], words[:, 256 * k + u : 256 * (k + 1) : 2], ident[:])
+        def widen(g, t, copy):
+            source, scale = j_raw[g][:, t, :].bitcast(FP8), column(scale_j, PACK * g + t)
+            if copy is VECTOR:
+                nc.vector.tensor_scalar(out=j_rows[g][:, t, :], in0=source, scalar1=scale, scalar2=None, op0=ALU.mult)
+            else:
+                nc.scalar.activation(out=j_rows[g][:, t, :], in_=source, func=ACT.Copy, scale=scale)
 
-        def regroup(i, c, copy):
-            if c == 0:
-                grouped_g[i] = work.tile([N, 2, 2 * N * 4], BF16, name=f"gg{i}", tag="gg", bufs=3, align_bytes=64)
+        def weave_j(g, copy, h):
+            weave(copy, j_woven[g], j_rows[g], *half_row(h))
+
+        def quantize_j(g):
+            quantize(cut(j_mx, slice(g * S, (g + 1) * S)), j_woven[g][:].rearrange("p n t -> p (n t)"))
+
+        turned, g_woven, g_mx, field_bank, total, product = {}, {}, {}, {}, {}, {}
+
+        def turn_rows(bank, slot, row, k_pass):
+            words = row.bitcast(F32)
+            for u in range(2):
+                w = slice(k_pass * PASS // 2 + u, (k_pass + 1) * PASS // 2, 2)
+                nc.tensor.transpose(bank[:, slot + u, :], words[:, w], ident[:])
+
+        def turn(i, c):
+            g, t = divmod(i, PACK)
+            turned[i, c] = psum.tile([LANES, 4, LANES], F32, name=f"turned{i}{c}", tag="early", bufs=4)
+            for k_pass in range(2):
+                turn_rows(turned[i, c], 2 * k_pass, g_sb[g][c][:, t, :], k_pass)
+
+        def regroup(woven, bank, copy):
             copy(
-                out=grouped_g[i][:, c, :].bitcast(F32).rearrange("p (k r u) -> p k r u", k=2, u=2),
-                in_=banks_t[i, c][:].rearrange("p (k u) r -> p k r u", k=2),
+                out=woven.bitcast(F32).rearrange("p (k n u) -> p k n u", k=2, u=2),
+                in_=bank[:].rearrange("p (k u) n -> p k n u", k=2),
             )
+
+        def regroup_g(i, c):
+            if i not in g_woven:
+                g_woven[i] = work.tile(
+                    [LANES, 2, 2 * PASS], BF16, name=f"g_woven{i}", tag="g_woven", bufs=3, align_bytes=64
+                )
+            regroup(g_woven[i][:, c, :], turned[i, c], SCALAR)
 
         def quantize_g(i):
-            codes = work.tile([N, 4 * N], U32, name=f"gc{i}", tag="gc", bufs=3, align_bytes=64)
-            planes = work.tile([N, 4 * N], U8, name=f"gp{i}", tag="gp", bufs=3, align_bytes=64)
-            codes_g[i] = (codes, planes)
-            quantize(codes[:], planes[:], grouped_g[i][:].rearrange("p c w -> p (c w)"))
+            g_mx[i] = (
+                work.tile([LANES, PASS], U32, name=f"g{i}_codes", tag="g_codes", bufs=3, align_bytes=64),
+                work.tile([LANES, PASS], U8, name=f"g{i}_scales", tag="g_scales", bufs=3, align_bytes=64),
+            )
+            quantize(everything(g_mx[i]), g_woven[i][:].rearrange("p c w -> p (c w)"))
 
         def field(i):
-            codes, planes = codes_g[i]
-            for c in range(2):
-                bank = psum.tile([N, S], F32, name=f"field{i}{c}", tag="acc", bufs=4)
-                banks_f[i, c] = bank
+            for c in (RE, IM):
+                field_bank[i, c] = psum.tile([LANES, S], F32, name=f"field{i}{c}", tag="late", bufs=4)
                 for k in range(2):
-                    w = slice((2 * c + k) * N, (2 * c + k + 1) * N)
-                    m = slice(k * S, (k + 1) * S)
-                    matmul(bank[:], (codes[:, w], planes[:, w]), (j_codes[:, m], j_planes[:, m]), k == 0, k == 1)
+                    w = slice((2 * c + k) * LANES, (2 * c + k + 1) * LANES)
+                    matmul(field_bank[i, c][:], cut(g_mx[i], w), cut(j_mx, slice(k * S, (k + 1) * S)), k == 0, k == 1)
+
+        def row_tile(name):
+            return work.tile([LANES, S], F32, name=name, tag="row", bufs=12)
 
         def add_e(i, c):
-            g, t = divmod(i, 4)
-            tile = work.tile([N, S], F32, name=f"t{i}{c}", tag=f"t{c}", bufs=3)
-            tot[i, c] = tile
-            nc.vector.tensor_tensor(out=tile[:], in0=banks_f[i, c][:], in1=e_sb[g][c][:, t, :], op=ALU.add)
+            g, t = divmod(i, PACK)
+            total[i, c] = row_tile(f"total{i}{c}")
+            nc.vector.tensor_tensor(out=total[i, c][:], in0=field_bank[i, c][:], in1=e_sb[g][c][:, t, :], op=ALU.add)
 
-        def scale_re(i):
-            for c, col in ((RE, cos_col(i)), (IM, sin_col(i))):
-                tile = work.tile([N, S], F32, name=f"q{i}{c}", tag=f"q{c}", bufs=3)
-                prod[i, c] = tile
-                nc.scalar.activation(out=tile[:], in_=tot[i, RE][:], func=ACT.Copy, scale=col)
+        def scale_re(i, c):
+            product[i, c] = row_tile(f"product{i}{c}")
+            nc.scalar.activation(
+                out=product[i, c][:], in_=total[i, RE][:], func=ACT.Copy, scale=(cosine(i), sine(i))[c]
+            )
 
-        def rotate(i):
-            g, t = divmod(i, 4)
-            for c, col in ((RE, neg_sin_col(i)), (IM, cos_col(i))):
-                if t == 0:
-                    fw[g, c] = planes_tile(f"fw{g}{c}")
-                nc.vector.scalar_tensor_tensor(
-                    out=fw[g, c][:, t, :], in0=tot[i, IM][:], scalar=col, in1=prod[i, c][:], op0=ALU.mult, op1=ALU.add
-                )
+        f_rows, f_woven = {}, {}
+        f_mx = {(g, c): quantized_pair(S, f"f{g}{c}") for g in range(HALVES) for c in (RE, IM)}
 
-        def weave_f(g, c, copy, c0, c1):
-            if c0 == 0:
-                fg[g, c] = woven_tile(f"fg{g}{c}")
-            weave(copy, fg[g, c], fw[g, c], c0, c1)
+        def rotate(i, c):
+            g, t = divmod(i, PACK)
+            if (g, c) not in f_rows:
+                f_rows[g, c] = rows_tile(f"f_rows{g}{c}")
+            nc.vector.scalar_tensor_tensor(
+                out=f_rows[g, c][:, t, :], in0=total[i, IM][:], scalar=(minus_sine(i), cosine(i))[c],
+                in1=product[i, c][:], op0=ALU.mult, op1=ALU.add,
+            )
+
+        def weave_f(g, c, copy, h):
+            if (g, c) not in f_woven:
+                f_woven[g, c] = woven_tile(f"f_woven{g}{c}")
+            weave(copy, f_woven[g, c], f_rows[g, c], *half_row(h))
 
         def quantize_f(g, c):
-            quantize(f_codes[g][c][:], f_planes[g][c][:], fg[g, c][:].rearrange("p s t -> p (s t)"))
+            quantize(everything(f_mx[g, c]), f_woven[g, c][:].rearrange("p n t -> p (n t)"))
 
-        bg = [keep.tile([N, 4, N, 4], BF16, name=f"bg{g}", align_bytes=64) for g in range(2)]
-        b_codes = [keep.tile([N, 4 * N], U32, name=f"bc{g}", align_bytes=64) for g in range(2)]
-        b_planes = [keep.tile([N, 4 * N], U8, name=f"bp{g}", align_bytes=64) for g in range(2)]
+        b_woven = [
+            keep.tile([LANES, PACK, LANES, PACK], BF16, name=f"b_woven{g}", align_bytes=64) for g in range(HALVES)
+        ]
+        b_mx = [quantized_pair(PASS, f"b{g}") for g in range(HALVES)]
 
-        def weave_b(g, copy, t0, t1):
-            copy(
-                out=bg[g][:, t0:t1],
-                in_=b_sb[:, :, 512 * g : 512 * (g + 1)].rearrange("p j (m t) -> p t m j", t=4)[:, t0:t1],
-            )
+        def weave_b(g, copy, h):
+            t = slice(2 * h, 2 * h + 2)
+            rows = b_sb[:, :, g * PASS : (g + 1) * PASS]
+            copy(out=b_woven[g][:, t], in_=rows.rearrange("p k (m t) -> p t m k", t=PACK)[:, t])
 
         def quantize_b(g):
-            quantize(b_codes[g][:], b_planes[g][:], bg[g][:].rearrange("p t m j -> p (t m j)"))
+            quantize(everything(b_mx[g]), b_woven[g][:].rearrange("p t m k -> p (t m k)"))
 
-        banks_a = {}
-        grouped_a = {}
-        codes_a = {}
+        a_turned, a_woven = {}, {}
+        a_mx = quantized_pair(D, "a")
 
-        def turn_a(c):
-            bank = psum.tile([N, 4, N], F32, name=f"turna{c}", tag="turn", bufs=4)
-            banks_a[c] = bank
+        def turn_a(q):
+            a_turned[q] = psum.tile([LANES, 4, LANES], F32, name=f"a_turned{q}", tag="early", bufs=4)
             for e in range(2):
-                words = a_sb[:, c, e, :].bitcast(F32)
-                for u in range(2):
-                    nc.tensor.transpose(bank[:, 2 * e + u, :], words[:, u:256:2], ident[:])
+                turn_rows(a_turned[q], 2 * e, a_sb[:, 2 * q + e, :], 0)
 
-        def regroup_a(c, copy):
-            tile = work.tile([N, 2 * N * 4], BF16, name=f"ag{c}", tag="ag", bufs=2, align_bytes=64)
-            grouped_a[c] = tile
-            copy(
-                out=tile[:].bitcast(F32).rearrange("p (e r u) -> p e r u", e=2, u=2),
-                in_=banks_a[c][:].rearrange("p (e u) r -> p e r u", e=2),
-            )
+        def regroup_a(q, copy):
+            h = q // 2
+            if h not in a_woven:
+                a_woven[h] = work.tile(
+                    [LANES, 2, 2 * PASS], BF16, name=f"a_woven{h}", tag="a_woven", bufs=1, align_bytes=64
+                )
+            regroup(a_woven[h][:, q % 2, :], a_turned[q], copy)
 
-        def quantize_a(c):
-            codes = keep.tile([N, 2 * N], U32, name=f"ac{c}", align_bytes=64)
-            planes = keep.tile([N, 2 * N], U8, name=f"ap{c}", align_bytes=64)
-            codes_a[c] = (codes, planes)
-            quantize(codes[:], planes[:], grouped_a[c][:])
+        def quantize_a(h):
+            w = slice(h * D // 2, (h + 1) * D // 2)
+            quantize(cut(a_mx, w), a_woven[h][:].rearrange("p q w -> p (q w)"))
 
-        banks_u = {}
-        th = {}
-        cw = {}
-        cg = {}
-        codes_c = {}
+        def width(c):
+            return LANES * len(CHUNKS[c])
+
+        u_row, tanh_rows, chi_rows, chi_woven, chi_mx = {}, {}, {}, {}, {}
 
         def material(c, g):
-            codes, planes = codes_a[c]
-            for h in range(2):
-                bank = psum.tile([N, 2, 2 * N], F32, name=f"u{c}{g}{h}", tag="turn", bufs=4)
-                banks_u[c, g, h] = bank
-                for e in range(2):
-                    w = slice((2 * h + e) * N, (2 * h + e + 1) * N)
-                    matmul(bank[:, e, :], (b_codes[g][:, w], b_planes[g][:, w]), (codes[:], planes[:]), True, True)
+            d = slice(CHUNKS[c][0] * LANES, CHUNKS[c][0] * LANES + width(c))
+            fit = 512 // width(c)
+            for h in range(PACK // fit):
+                bank = psum.tile([LANES, fit, width(c)], F32, name=f"u{c}{g}{h}", tag="early", bufs=4)
+                for e in range(fit):
+                    t = h * fit + e
+                    u_row[c, g, t] = bank[:, e, :]
+                    m = slice(t * LANES, (t + 1) * LANES)
+                    matmul(bank[:, e, :], cut(b_mx[g], m), cut(a_mx, d), True, True)
 
         def tanh_u(c, g):
-            tile = work.tile([N, 4, 2 * N], F32, name=f"th{c}{g}", tag="th", bufs=3)
-            th[c, g] = tile
-            for t in range(4):
+            tanh_rows[c, g] = work.tile([LANES, PACK, width(c)], F32, name=f"tanh{c}{g}", tag="tanh", bufs=2)
+            for t in range(PACK):
                 nc.scalar.activation(
-                    out=tile[:, t, :], in_=banks_u[c, g, t // 2][:, t % 2, :], func=ACT.Tanh,
-                    bias=bias_u[:, 4 * g + t : 4 * g + t + 1],
+                    out=tanh_rows[c, g][:, t, :], in_=u_row[c, g, t], func=ACT.Tanh, bias=column(tanh_bias, PACK * g + t)
                 )
 
         def affine(c, g):
-            tile = work.tile([N, 4, 2 * N], BF16, name=f"cw{c}{g}", tag="cw", bufs=3, align_bytes=64)
-            cw[c, g] = tile
-            for t in range(4):
-                i = 4 * g + t
+            chi_rows[c, g] = work.tile(
+                [LANES, PACK, width(c)], BF16, name=f"chi_rows{c}{g}", tag="chi_rows", bufs=2, align_bytes=64
+            )
+            for t in range(PACK):
+                i = PACK * g + t
                 nc.vector.tensor_scalar(
-                    out=tile[:, t, :], in0=th[c, g][:, t, :], scalar1=vol2[:, i : i + 1], scalar2=vol1[:, i : i + 1],
-                    op0=ALU.mult, op1=ALU.add,
+                    out=chi_rows[c, g][:, t, :], in0=tanh_rows[c, g][:, t, :], scalar1=column(vol_2, i),
+                    scalar2=column(vol_1, i), op0=ALU.mult, op1=ALU.add,
                 )
 
         def weave_c(c, g, copy):
-            tile = work.tile([N, 2 * N, 4], BF16, name=f"cg{c}{g}", tag="cg", bufs=3, align_bytes=64)
-            cg[c, g] = tile
-            weave(copy, tile, cw[c, g], 0, 2 * N)
+            chi_woven[c, g] = work.tile(
+                [LANES, width(c), PACK], BF16, name=f"chi_woven{c}{g}", tag="chi_woven", bufs=2, align_bytes=64
+            )
+            weave(copy, chi_woven[c, g], chi_rows[c, g], 0, width(c))
 
         def quantize_c(c, g):
-            codes = keep.tile([N, 2 * N], U32, name=f"cc{c}{g}", align_bytes=64)
-            planes = keep.tile([N, 2 * N], U8, name=f"cp{c}{g}", align_bytes=64)
-            codes_c[c, g] = (codes, planes)
-            quantize(codes[:], planes[:], cg[c, g][:].rearrange("p s t -> p (s t)"))
+            chi_mx[c, g] = quantized_pair(width(c), f"chi{c}{g}")
+            quantize(everything(chi_mx[c, g]), chi_woven[c, g][:].rearrange("p n t -> p (n t)"))
 
-        banks_m = {}
-        res = {}
-        out_view = [x.rearrange("(c p e) s -> c p e s", p=N, e=2) for x in (out_0, out_1)]
+        moment_bank = {}
 
         def moment(c, e, k):
-            bank = psum.tile([N, S], F32, name=f"m{c}{e}{k}", tag="acc", bufs=4)
-            banks_m[c, e, k] = bank
-            w = slice(e * N, (e + 1) * N)
-            for g in range(2):
-                codes, planes = codes_c[c, g]
-                matmul(bank[:], (codes[:, w], planes[:, w]), (f_codes[g][k][:], f_planes[g][k][:]), g == 0, g == 1)
+            moment_bank[c, e, k] = psum.tile([LANES, S], F32, name=f"moment{c}{e}{k}", tag="late", bufs=4)
+            w = slice(e * LANES, (e + 1) * LANES)
+            for g in range(HALVES):
+                matmul(moment_bank[c, e, k][:], cut(chi_mx[c, g], w), everything(f_mx[g, k]), g == 0, g == HALVES - 1)
 
         def empty(c, e, k, copy):
-            if e == 0:
-                res[c, k] = work.tile([N, 2, S], F32, name=f"res{c}{k}", tag=f"res{k}", bufs=2)
-            copy(out=res[c, k][:, e, :], in_=banks_m[c, e, k][:])
+            n = CHUNKS[c][e]
+            result = row_tile(f"result{n}{k}")
+            copy(out=result[:], in_=moment_bank[c, e, k][:])
+            nc.sync.dma_start(out=(out_0, out_1)[k][n * LANES : (n + 1) * LANES, :], in_=result[:])
 
-        def store(c, k):
-            nc.sync.dma_start(out=out_view[k][c], in_=res[c, k][:])
 
-        V, A = nc.vector.tensor_copy, nc.scalar.copy
-
-        for t in range(4):
-            widen_v(0, t)
-        turn(0)
-        turn(1)
-        regroup(0, RE, A)
-        regroup(0, IM, A)
-        weave(V, jg[0], jw[0], 0, S)
-        widen_v(1, 0)
-        widen_v(1, 1)
-        widen_s(1, 2)
-        widen_s(1, 3)
-        regroup(1, RE, A)
-        regroup(1, IM, A)
-        quantize(j_codes[:, :S], j_planes[:, :S], jg[0][:].rearrange("p s t -> p (s t)"))
-        weave(V, jg[1], jw[1], 0, S)
-        quantize_g(0)
-        quantize(j_codes[:, S:], j_planes[:, S:], jg[1][:].rearrange("p s t -> p (s t)"))
-        nc.vector.tensor_scalar(
-            out=bias_u[:], in0=host_flat, scalar1=-0.5 * math.log(3.0), scalar2=None, op0=ALU.add
+        pipeline = (
+            (lambda i: regroup_g(i, RE), 2),
+            (lambda i: rotate(i, IM), -1),
+            (lambda i: turn(i, IM), 2),
+            (lambda i: add_e(i, RE), 0),
+            (quantize_g, 1),
+            (lambda i: turn(i, RE), 3),
+            (lambda i: scale_re(i, IM), 0),
+            (lambda i: scale_re(i, RE), 0),
+            (field, 1),
+            (lambda i: add_e(i, IM), 0),
+            (lambda i: rotate(i, RE), -1),
+            (lambda i: regroup_g(i, IM), 2),
         )
-        nc.vector.tensor_scalar(out=vol2[:], in0=vol_flat, scalar1=2.0, scalar2=None, op0=ALU.mult)
-        nc.vector.tensor_copy(out=vol1[:], in_=vol_flat)
-        field(0)
-        turn(2)
 
-        def step(i):
-            if i < 7:
-                quantize_g(i + 1)
-                field(i + 1)
-            if i + 3 < 8:
-                turn(i + 3)
-            if i < 8:
-                add_e(i, RE)
-                add_e(i, IM)
-            if i >= 1:
-                scale_re(i - 1)
-            if i + 2 < 8:
-                regroup(i + 2, RE, A)
-                regroup(i + 2, IM, A)
-            if i >= 1:
-                rotate(i - 1)
+        def step(s):
+            for unit, ahead in pipeline:
+                if 0 <= s + ahead < TILES:
+                    unit(s + ahead)
 
+        widen(0, 0, SCALAR)
+        widen(0, 1, SCALAR)
+        widen(0, 2, VECTOR)
+        widen(0, 3, VECTOR)
+        material_constants()
+        step(-3)
+        widen(1, 0, VECTOR)
+        widen(1, 1, SCALAR)
+        widen(1, 2, VECTOR)
+        widen(1, 3, VECTOR)
+        weave_j(0, VECTOR, 1)
+        weave_j(1, VECTOR, 0)
+        weave_j(1, SCALAR, 1)
+        step(-2)
+        weave_j(0, VECTOR, 0)
+        quantize_j(0)
+        quantize_j(1)
+        step(-1)
+
+        weave_b(0, SCALAR, 0)
+        weave_b(0, VECTOR, 1)
         step(0)
-        step(1)
-        weave_b(0, A, 0, 2)
-        step(2)
-        weave_b(0, A, 2, 4)
-        step(3)
-        weave_b(1, A, 0, 2)
         quantize_b(0)
-        step(4)
-        weave_b(1, A, 2, 4)
-        weave_f(0, RE, V, 0, S // 2)
+        weave_b(1, SCALAR, 0)
+        step(1)
+        step(2)
         turn_a(0)
-        turn_a(1)
-        step(5)
+        weave_b(1, SCALAR, 1)
+        step(3)
+        regroup_a(0, SCALAR)
         quantize_b(1)
-        weave_f(0, RE, A, S // 2, S)
-        regroup_a(0, A)
-        regroup_a(1, A)
+        step(4)
+        turn_a(1)
+        weave_f(0, RE, SCALAR, 0)
+        weave_f(0, RE, VECTOR, 1)
+        weave_f(0, IM, SCALAR, 0)
+        regroup_a(1, SCALAR)
+        step(5)
+        turn_a(2)
+        turn_a(3)
+        weave_f(0, IM, SCALAR, 1)
         quantize_a(0)
+        quantize_f(0, RE)
+        regroup_a(2, SCALAR)
+        regroup_a(3, SCALAR)
         material(0, 0)
         step(6)
         quantize_a(1)
-        quantize_f(0, RE)
-        weave_f(0, IM, V, 0, S // 2)
         tanh_u(0, 0)
-        material(0, 1)
-        weave_f(0, IM, A, S // 2, S)
         step(7)
         affine(0, 0)
-        tanh_u(0, 1)
-        quantize_f(0, IM)
-        weave_c(0, 0, V)
         step(8)
-        affine(0, 1)
-        quantize_c(0, 0)
-        weave_f(1, RE, V, 0, S)
-        turn_a(2)
-        turn_a(3)
-        regroup_a(2, A)
-        regroup_a(3, A)
-        weave_f(1, IM, V, 0, S)
-        quantize_f(1, RE)
-        material(1, 0)
-        tanh_u(1, 0)
-        weave_c(0, 1, V)
-        quantize_f(1, IM)
-        quantize_a(2)
-        material(1, 1)
-        tanh_u(1, 1)
-        quantize_c(0, 1)
-        quantize_a(3)
 
-        for c in range(4):
-            last = c == 3
-            moment(c, 0, RE)
-            moment(c, 0, IM)
-            moment(c, 1, RE)
-            moment(c, 1, IM)
-            if not last:
-                affine(c + 1, 0)
-                affine(c + 1, 1)
-                weave_c(c + 1, 0, V)
-            if c + 2 < 4:
-                material(c + 2, 0)
-            empty(c, 0, RE, A)
-            empty(c, 0, IM, V if last else A)
-            if not last:
-                weave_c(c + 1, 1, V)
-                quantize_c(c + 1, 0)
-            if c + 2 < 4:
-                tanh_u(c + 2, 0)
-                material(c + 2, 1)
-            empty(c, 1, RE, A)
-            store(c, RE)
-            empty(c, 1, IM, V if last else A)
-            store(c, IM)
-            if not last:
-                quantize_c(c + 1, 1)
-            if c + 2 < 4:
-                tanh_u(c + 2, 1)
+        material(0, 1)
+        tanh_u(0, 1)
+        material(1, 0)
+        material(1, 1)
+        weave_c(0, 0, VECTOR)
+        affine(0, 1)
+        weave_f(1, RE, VECTOR, 0)
+        weave_f(1, RE, SCALAR, 1)
+        weave_c(0, 1, VECTOR)
+        tanh_u(1, 0)
+        affine(1, 0)
+        tanh_u(1, 1)
+        material(2, 0)
+        material(2, 1)
+        quantize_c(0, 0)
+        quantize_c(0, 1)
+        weave_f(1, IM, SCALAR, 0)
+        weave_f(1, IM, SCALAR, 1)
+        quantize_f(1, RE)
+
+        for e in range(4):
+            moment(0, e, RE)
+        tanh_u(2, 0)
+        for e in range(4):
+            empty(0, e, RE, SCALAR)
+        quantize_f(0, IM)
+        quantize_f(1, IM)
+        affine(1, 1)
+        weave_c(1, 0, VECTOR)
+        moment(0, 0, IM)
+        weave_c(1, 1, VECTOR)
+        quantize_c(1, 0)
+        moment(0, 1, IM)
+        empty(0, 0, IM, SCALAR)
+        tanh_u(2, 1)
+        moment(0, 2, IM)
+        quantize_c(1, 1)
+        affine(2, 0)
+        moment(0, 3, IM)
+        moment(1, 0, RE)
+        affine(2, 1)
+        empty(0, 1, IM, SCALAR)
+        empty(0, 2, IM, SCALAR)
+        moment(1, 0, IM)
+        empty(0, 3, IM, SCALAR)
+
+        empty(1, 0, RE, SCALAR)
+        moment(1, 1, RE)
+        weave_c(2, 0, VECTOR)
+        weave_c(2, 1, VECTOR)
+        quantize_c(2, 0)
+        empty(1, 0, IM, SCALAR)
+        quantize_c(2, 1)
+        empty(1, 1, RE, SCALAR)
+        moment(1, 1, IM)
+        moment(2, 0, RE)
+        empty(1, 1, IM, VECTOR)
+        moment(2, 0, IM)
+        empty(2, 0, RE, VECTOR)
+        moment(2, 1, RE)
+        empty(2, 0, IM, SCALAR)
+        moment(2, 1, IM)
+        empty(2, 1, RE, SCALAR)
+        empty(2, 1, IM, SCALAR)

import math
from contextlib import ExitStack

import concourse.mybir as mybir
from concourse.masks import make_identity

P, Q, S, R, D = 1024, 1024, 512, 512, 1024
FLOPS = 2 * (2 * P * Q * S + D * R * P + 2 * D * P * S)

F32 = mybir.dt.float32
BF16 = mybir.dt.bfloat16
U32 = mybir.dt.uint32
U8 = mybir.dt.uint8
FP8 = mybir.dt.float8_e4m3fn
FP8X4 = mybir.dt.float8_e4m3fn_x4
ALU = mybir.AluOpType
ACT = mybir.ActivationFunctionType

LANES = 128
PACK = 4
PASS = LANES * PACK
HALVES = P // PASS
TILES = P // LANES
RE, IM = 0, 1

CHUNKS = ((0, 1, 2, 3), (4, 5), (6, 7))


def tile_green_material_moments_f5_kernel(
    tc, g_re, g_im, j_bytes, j_scale, e0_re, e0_im, phi, a, b, host, vol, out_0, out_1
):
    nc = tc.nc
    with ExitStack() as ctx:
        keep = ctx.enter_context(tc.tile_pool(name="keep", bufs=1))
        work = ctx.enter_context(tc.tile_pool(name="work", bufs=2))
        psum = ctx.enter_context(tc.psum_pool(name="psum", bufs=4))
        ctx.enter_context(tc.manual_schedule())

        def load_cells(source, dtype, name):
            tile = keep.tile([LANES, TILES], dtype, name=name)
            nc.scalar.dma_start(
                out=tile[:].rearrange("p (g t) -> p g t", t=PACK),
                in_=source.rearrange("(g p t) -> p g t", p=LANES, t=PACK),
            )
            return tile

        scale_j = load_cells(j_scale.rearrange("k o -> (k o)"), F32, "scale_j")
        phi_sb = load_cells(phi, BF16, "phi_sb")
        host_sb = load_cells(host, BF16, "host_sb")
        vol_sb = load_cells(vol, BF16, "vol_sb")

        def four_rows(source):
            return source.rearrange("(g p t) n -> g p t n", p=LANES, t=PACK)

        j_raw = [keep.tile([LANES, PACK, S], U8, name=f"j_raw{g}", align_bytes=64) for g in range(HALVES)]
        g_sb = [
            [keep.tile([LANES, PACK, Q], BF16, name=f"g_sb{g}{c}", align_bytes=64) for c in (RE, IM)]
            for g in range(HALVES)
        ]
        e_sb = [
            [keep.tile([LANES, PACK, S], BF16, name=f"e_sb{g}{c}", align_bytes=64) for c in (RE, IM)]
            for g in range(HALVES)
        ]
        a_sb = keep.tile([LANES, D // LANES, R], BF16, name="a_sb", align_bytes=64)
        b_sb = keep.tile([LANES, PACK, P], BF16, name="b_sb", align_bytes=64)

        def load_rows(tiles, sources, g, t0, t1):
            for c in (RE, IM):
                nc.sync.dma_start(out=tiles[g][c][:, t0:t1, :], in_=four_rows(sources[c])[g][:, t0:t1, :])

        def load_g(g, t0, t1):
            load_rows(g_sb, (g_re, g_im), g, t0, t1)

        def load_e(g, t0, t1):
            load_rows(e_sb, (e0_re, e0_im), g, t0, t1)

        def load_b(g):
            w = slice(g * PASS, (g + 1) * PASS)
            nc.sync.dma_start(out=b_sb[:, :, w], in_=four_rows(b)[0][:, :, w])

        def load_a(n0, n1):
            nc.sync.dma_start(out=a_sb[:, n0:n1, :], in_=a.rearrange("(n p) r -> p n r", p=LANES)[:, n0:n1, :])

        for g in range(HALVES):
            nc.sync.dma_start(out=j_raw[g][:], in_=four_rows(j_bytes)[g])
        load_g(0, 0, 1)
        load_g(0, 1, 2)
        load_e(0, 0, 2)
        load_g(0, 2, 3)
        load_b(0)
        load_b(1)
        load_g(0, 3, 4)
        load_a(0, 4)
        load_e(0, 2, 4)
        load_g(1, 0, 1)
        load_g(1, 1, 2)
        load_e(1, 0, 2)
        load_g(1, 2, 4)
        load_e(1, 2, 4)
        load_a(4, 8)

        ident = keep.tile([LANES, LANES], F32, name="ident")
        make_identity(nc, ident[:])

        zero = keep.tile([LANES, 1], F32, name="zero")
        first_use = keep.tile([LANES, 2], F32, name="first_use")
        nc.vector.memset(zero[:], 0.0)
        nc.scalar.activation(out=first_use[:, 0:1], in_=zero[:], func=ACT.Sin)

        angle = keep.tile([LANES, 3, TILES], F32, name="angle")
        trig = keep.tile([LANES, 3, TILES], F32, name="trig")
        magnitude = keep.tile([LANES, TILES], F32, name="magnitude")
        nc.vector.tensor_copy(out=angle[:, 0, :], in_=phi_sb[:])
        nc.vector.tensor_scalar(out=angle[:, 2, :], in0=phi_sb[:], scalar1=-1.0, scalar2=None, op0=ALU.mult)
        nc.vector.tensor_tensor(out=magnitude[:], in0=angle[:, 0, :], in1=angle[:, 2, :], op=ALU.max)
        nc.vector.tensor_scalar(
            out=angle[:, 1, :], in0=magnitude[:], scalar1=-1.0, scalar2=math.pi / 2, op0=ALU.mult, op1=ALU.add
        )
        nc.scalar.activation(
            out=trig[:].rearrange("p k i -> p (k i)"), in_=angle[:].rearrange("p k i -> p (k i)"), func=ACT.Sin
        )
        nc.scalar.activation(out=first_use[:, 1:2], in_=zero[:], func=ACT.Tanh)

        def column(tile, i):
            return tile[:, i : i + 1]

        def sine(i):
            return column(trig[:, 0, :], i)

        def cosine(i):
            return column(trig[:, 1, :], i)

        def minus_sine(i):
            return column(trig[:, 2, :], i)

        tanh_bias = keep.tile([LANES, TILES], F32, name="tanh_bias")
        vol_1 = keep.tile([LANES, TILES], F32, name="vol_1")
        vol_2 = keep.tile([LANES, TILES], F32, name="vol_2")

        def material_constants():
            nc.vector.tensor_scalar(
                out=tanh_bias[:], in0=host_sb[:], scalar1=-0.5 * math.log(3.0), scalar2=None, op0=ALU.add
            )
            nc.vector.tensor_scalar(out=vol_2[:], in0=vol_sb[:], scalar1=2.0, scalar2=None, op0=ALU.mult)
            nc.vector.tensor_copy(out=vol_1[:], in_=vol_sb[:])

        VECTOR, SCALAR = nc.vector.tensor_copy, nc.scalar.copy

        def rows_tile(name):
            return work.tile([LANES, PACK, S], BF16, name=name, tag="rows", bufs=4, align_bytes=64)

        def woven_tile(name):
            return work.tile([LANES, S, PACK], BF16, name=name, tag="woven", bufs=4, align_bytes=64)

        def weave(copy, woven, rows, n0, n1):
            copy(
                out=woven[:, n0:n1, :].rearrange("p (n i) t -> p n t i", i=4),
                in_=rows[:, :, n0:n1].rearrange("p t (n i) -> p n t i", i=4),
            )

        def half_row(h):
            return h * S // 2, (h + 1) * S // 2

        def quantized_pair(columns, name):
            return (
                keep.tile([LANES, columns], U32, name=f"{name}_codes", align_bytes=64),
                keep.tile([LANES, columns], U8, name=f"{name}_scales", align_bytes=64),
            )

        def cut(pair, w):
            return pair[0][:, w], pair[1][:, w]

        def everything(pair):
            return pair[0][:], pair[1][:]

        def quantize(pair, woven):
            nc.vector.quantize_mx(out=pair[0].bitcast(FP8X4), scales=pair[1], in_=woven)

        def matmul(out, lhs, rhs, first, last):
            nc.tensor.matmul_mx(
                out=out, lhsT=lhs[0].bitcast(FP8X4), lhsT_scale=lhs[1], rhs=rhs[0].bitcast(FP8X4), rhs_scale=rhs[1],
                start=first, stop=last,
            )

        j_rows = [rows_tile(f"j_rows{g}") for g in range(HALVES)]
        j_woven = [woven_tile(f"j_woven{g}") for g in range(HALVES)]
        j_mx = quantized_pair(HALVES * S, "j")

        def widen(g, t, copy):
            source, scale = j_raw[g][:, t, :].bitcast(FP8), column(scale_j, PACK * g + t)
            if copy is VECTOR:
                nc.vector.tensor_scalar(out=j_rows[g][:, t, :], in0=source, scalar1=scale, scalar2=None, op0=ALU.mult)
            else:
                nc.scalar.activation(out=j_rows[g][:, t, :], in_=source, func=ACT.Copy, scale=scale)

        def weave_j(g, copy, h):
            weave(copy, j_woven[g], j_rows[g], *half_row(h))

        def quantize_j(g):
            quantize(cut(j_mx, slice(g * S, (g + 1) * S)), j_woven[g][:].rearrange("p n t -> p (n t)"))

        turned, g_woven, g_mx, field_bank, total, product = {}, {}, {}, {}, {}, {}

        def turn_rows(bank, slot, row, k_pass):
            words = row.bitcast(F32)
            for u in range(2):
                w = slice(k_pass * PASS // 2 + u, (k_pass + 1) * PASS // 2, 2)
                nc.tensor.transpose(bank[:, slot + u, :], words[:, w], ident[:])

        def turn(i, c):
            g, t = divmod(i, PACK)
            turned[i, c] = psum.tile([LANES, 4, LANES], F32, name=f"turned{i}{c}", tag="early", bufs=4)
            for k_pass in range(2):
                turn_rows(turned[i, c], 2 * k_pass, g_sb[g][c][:, t, :], k_pass)

        def regroup(woven, bank, copy):
            copy(
                out=woven.bitcast(F32).rearrange("p (k n u) -> p k n u", k=2, u=2),
                in_=bank[:].rearrange("p (k u) n -> p k n u", k=2),
            )

        def regroup_g(i, c):
            if i not in g_woven:
                g_woven[i] = work.tile(
                    [LANES, 2, 2 * PASS], BF16, name=f"g_woven{i}", tag="g_woven", bufs=3, align_bytes=64
                )
            regroup(g_woven[i][:, c, :], turned[i, c], SCALAR)

        def quantize_g(i):
            g_mx[i] = (
                work.tile([LANES, PASS], U32, name=f"g{i}_codes", tag="g_codes", bufs=3, align_bytes=64),
                work.tile([LANES, PASS], U8, name=f"g{i}_scales", tag="g_scales", bufs=3, align_bytes=64),
            )
            quantize(everything(g_mx[i]), g_woven[i][:].rearrange("p c w -> p (c w)"))

        def field(i):
            for c in (RE, IM):
                field_bank[i, c] = psum.tile([LANES, S], F32, name=f"field{i}{c}", tag="late", bufs=4)
                for k in range(2):
                    w = slice((2 * c + k) * LANES, (2 * c + k + 1) * LANES)
                    matmul(field_bank[i, c][:], cut(g_mx[i], w), cut(j_mx, slice(k * S, (k + 1) * S)), k == 0, k == 1)

        def row_tile(name):
            return work.tile([LANES, S], F32, name=name, tag="row", bufs=12)

        def add_e(i, c):
            g, t = divmod(i, PACK)
            total[i, c] = row_tile(f"total{i}{c}")
            nc.vector.tensor_tensor(out=total[i, c][:], in0=field_bank[i, c][:], in1=e_sb[g][c][:, t, :], op=ALU.add)

        def scale_re(i, c):
            product[i, c] = row_tile(f"product{i}{c}")
            nc.scalar.activation(
                out=product[i, c][:], in_=total[i, RE][:], func=ACT.Copy, scale=(cosine(i), sine(i))[c]
            )

        f_rows, f_woven = {}, {}
        f_mx = {(g, c): quantized_pair(S, f"f{g}{c}") for g in range(HALVES) for c in (RE, IM)}

        def rotate(i, c):
            g, t = divmod(i, PACK)
            if (g, c) not in f_rows:
                f_rows[g, c] = rows_tile(f"f_rows{g}{c}")
            nc.vector.scalar_tensor_tensor(
                out=f_rows[g, c][:, t, :], in0=total[i, IM][:], scalar=(minus_sine(i), cosine(i))[c],
                in1=product[i, c][:], op0=ALU.mult, op1=ALU.add,
            )

        def weave_f(g, c, copy, h):
            if (g, c) not in f_woven:
                f_woven[g, c] = woven_tile(f"f_woven{g}{c}")
            weave(copy, f_woven[g, c], f_rows[g, c], *half_row(h))

        def quantize_f(g, c):
            quantize(everything(f_mx[g, c]), f_woven[g, c][:].rearrange("p n t -> p (n t)"))

        b_woven = [
            keep.tile([LANES, PACK, LANES, PACK], BF16, name=f"b_woven{g}", align_bytes=64) for g in range(HALVES)
        ]
        b_mx = [quantized_pair(PASS, f"b{g}") for g in range(HALVES)]

        def weave_b(g, copy, h):
            t = slice(2 * h, 2 * h + 2)
            rows = b_sb[:, :, g * PASS : (g + 1) * PASS]
            copy(out=b_woven[g][:, t], in_=rows.rearrange("p k (m t) -> p t m k", t=PACK)[:, t])

        def quantize_b(g):
            quantize(everything(b_mx[g]), b_woven[g][:].rearrange("p t m k -> p (t m k)"))

        a_turned, a_woven = {}, {}
        a_mx = quantized_pair(D, "a")

        def turn_a(q):
            a_turned[q] = psum.tile([LANES, 4, LANES], F32, name=f"a_turned{q}", tag="early", bufs=4)
            for e in range(2):
                turn_rows(a_turned[q], 2 * e, a_sb[:, 2 * q + e, :], 0)

        def regroup_a(q, copy):
            h = q // 2
            if h not in a_woven:
                a_woven[h] = work.tile(
                    [LANES, 2, 2 * PASS], BF16, name=f"a_woven{h}", tag="a_woven", bufs=1, align_bytes=64
                )
            regroup(a_woven[h][:, q % 2, :], a_turned[q], copy)

        def quantize_a(h):
            w = slice(h * D // 2, (h + 1) * D // 2)
            quantize(cut(a_mx, w), a_woven[h][:].rearrange("p q w -> p (q w)"))

        def width(c):
            return LANES * len(CHUNKS[c])

        u_row, tanh_rows, chi_rows, chi_woven, chi_mx = {}, {}, {}, {}, {}

        def material(c, g):
            d = slice(CHUNKS[c][0] * LANES, CHUNKS[c][0] * LANES + width(c))
            fit = 512 // width(c)
            for h in range(PACK // fit):
                bank = psum.tile([LANES, fit, width(c)], F32, name=f"u{c}{g}{h}", tag="early", bufs=4)
                for e in range(fit):
                    t = h * fit + e
                    u_row[c, g, t] = bank[:, e, :]
                    m = slice(t * LANES, (t + 1) * LANES)
                    matmul(bank[:, e, :], cut(b_mx[g], m), cut(a_mx, d), True, True)

        def tanh_u(c, g):
            tanh_rows[c, g] = work.tile([LANES, PACK, width(c)], F32, name=f"tanh{c}{g}", tag="tanh", bufs=2)
            for t in range(PACK):
                nc.scalar.activation(
                    out=tanh_rows[c, g][:, t, :], in_=u_row[c, g, t], func=ACT.Tanh, bias=column(tanh_bias, PACK * g + t)
                )

        def affine(c, g):
            chi_rows[c, g] = work.tile(
                [LANES, PACK, width(c)], BF16, name=f"chi_rows{c}{g}", tag="chi_rows", bufs=2, align_bytes=64
            )
            for t in range(PACK):
                i = PACK * g + t
                nc.vector.tensor_scalar(
                    out=chi_rows[c, g][:, t, :], in0=tanh_rows[c, g][:, t, :], scalar1=column(vol_2, i),
                    scalar2=column(vol_1, i), op0=ALU.mult, op1=ALU.add,
                )

        def weave_c(c, g, copy):
            chi_woven[c, g] = work.tile(
                [LANES, width(c), PACK], BF16, name=f"chi_woven{c}{g}", tag="chi_woven", bufs=2, align_bytes=64
            )
            weave(copy, chi_woven[c, g], chi_rows[c, g], 0, width(c))

        def quantize_c(c, g):
            chi_mx[c, g] = quantized_pair(width(c), f"chi{c}{g}")
            quantize(everything(chi_mx[c, g]), chi_woven[c, g][:].rearrange("p n t -> p (n t)"))

        moment_bank = {}

        def moment(c, e, k):
            moment_bank[c, e, k] = psum.tile([LANES, S], F32, name=f"moment{c}{e}{k}", tag="late", bufs=4)
            w = slice(e * LANES, (e + 1) * LANES)
            for g in range(HALVES):
                matmul(moment_bank[c, e, k][:], cut(chi_mx[c, g], w), everything(f_mx[g, k]), g == 0, g == HALVES - 1)

        def empty(c, e, k, copy):
            n = CHUNKS[c][e]
            result = row_tile(f"result{n}{k}")
            copy(out=result[:], in_=moment_bank[c, e, k][:])
            nc.sync.dma_start(out=(out_0, out_1)[k][n * LANES : (n + 1) * LANES, :], in_=result[:])


        pipeline = (
            (lambda i: regroup_g(i, RE), 2),
            (lambda i: rotate(i, IM), -1),
            (lambda i: turn(i, IM), 2),
            (lambda i: add_e(i, RE), 0),
            (quantize_g, 1),
            (lambda i: turn(i, RE), 3),
            (lambda i: scale_re(i, IM), 0),
            (lambda i: scale_re(i, RE), 0),
            (field, 1),
            (lambda i: add_e(i, IM), 0),
            (lambda i: rotate(i, RE), -1),
            (lambda i: regroup_g(i, IM), 2),
        )

        def step(s):
            for unit, ahead in pipeline:
                if 0 <= s + ahead < TILES:
                    unit(s + ahead)

        widen(0, 0, SCALAR)
        widen(0, 1, SCALAR)
        widen(0, 2, VECTOR)
        widen(0, 3, VECTOR)
        material_constants()
        step(-3)
        widen(1, 0, VECTOR)
        widen(1, 1, SCALAR)
        widen(1, 2, VECTOR)
        widen(1, 3, VECTOR)
        weave_j(0, VECTOR, 1)
        weave_j(1, VECTOR, 0)
        weave_j(1, SCALAR, 1)
        step(-2)
        weave_j(0, VECTOR, 0)
        quantize_j(0)
        quantize_j(1)
        step(-1)

        weave_b(0, SCALAR, 0)
        weave_b(0, VECTOR, 1)
        step(0)
        quantize_b(0)
        weave_b(1, SCALAR, 0)
        step(1)
        step(2)
        turn_a(0)
        weave_b(1, SCALAR, 1)
        step(3)
        regroup_a(0, SCALAR)
        quantize_b(1)
        step(4)
        turn_a(1)
        weave_f(0, RE, SCALAR, 0)
        weave_f(0, RE, VECTOR, 1)
        weave_f(0, IM, SCALAR, 0)
        regroup_a(1, SCALAR)
        step(5)
        turn_a(2)
        turn_a(3)
        weave_f(0, IM, SCALAR, 1)
        quantize_a(0)
        quantize_f(0, RE)
        regroup_a(2, SCALAR)
        regroup_a(3, SCALAR)
        material(0, 0)
        step(6)
        quantize_a(1)
        tanh_u(0, 0)
        step(7)
        affine(0, 0)
        step(8)

        material(0, 1)
        tanh_u(0, 1)
        material(1, 0)
        material(1, 1)
        weave_c(0, 0, VECTOR)
        affine(0, 1)
        weave_f(1, RE, VECTOR, 0)
        weave_f(1, RE, SCALAR, 1)
        weave_c(0, 1, VECTOR)
        tanh_u(1, 0)
        affine(1, 0)
        tanh_u(1, 1)
        material(2, 0)
        material(2, 1)
        quantize_c(0, 0)
        quantize_c(0, 1)
        weave_f(1, IM, SCALAR, 0)
        weave_f(1, IM, SCALAR, 1)
        quantize_f(1, RE)

        for e in range(4):
            moment(0, e, RE)
        tanh_u(2, 0)
        for e in range(4):
            empty(0, e, RE, SCALAR)
        quantize_f(0, IM)
        quantize_f(1, IM)
        affine(1, 1)
        weave_c(1, 0, VECTOR)
        moment(0, 0, IM)
        weave_c(1, 1, VECTOR)
        quantize_c(1, 0)
        moment(0, 1, IM)
        empty(0, 0, IM, SCALAR)
        tanh_u(2, 1)
        moment(0, 2, IM)
        quantize_c(1, 1)
        affine(2, 0)
        moment(0, 3, IM)
        moment(1, 0, RE)
        affine(2, 1)
        empty(0, 1, IM, SCALAR)
        empty(0, 2, IM, SCALAR)
        moment(1, 0, IM)
        empty(0, 3, IM, SCALAR)

        empty(1, 0, RE, SCALAR)
        moment(1, 1, RE)
        weave_c(2, 0, VECTOR)
        weave_c(2, 1, VECTOR)
        quantize_c(2, 0)
        empty(1, 0, IM, SCALAR)
        quantize_c(2, 1)
        empty(1, 1, RE, SCALAR)
        moment(1, 1, IM)
        moment(2, 0, RE)
        empty(1, 1, IM, VECTOR)
        moment(2, 0, IM)
        empty(2, 0, RE, VECTOR)
        moment(2, 1, RE)
        empty(2, 0, IM, SCALAR)
        moment(2, 1, IM)
        empty(2, 1, RE, SCALAR)
        empty(2, 1, IM, SCALAR)
